import numpy as np
import ml_dtypes


def mxq(x, axis, fmt="e4m3"):
    dtype, down = {"e4m3": (ml_dtypes.float8_e4m3fn, 7), "e5m2": (ml_dtypes.float8_e5m2, 14)}[fmt]
    v = np.moveaxis(np.asarray(x, np.float32).astype(ml_dtypes.bfloat16).astype(np.float64), axis, -1)
    blocks = v.reshape(v.shape[:-1] + (-1, 32))
    amax = np.abs(blocks).max(-1, keepdims=True)
    byte = np.maximum(np.where(amax > 0, np.frexp(amax)[1] - 1 + 127, 0) - down, 1)
    scale = np.exp2(byte - 127.0)
    codes = (blocks / scale).astype(np.float32).astype(dtype).astype(np.float64)
    return np.moveaxis((codes * scale).reshape(v.shape), -1, axis)


WIDE = False


def mx_kscale(k):
    if not WIDE:
        return np.ones(k)
    levels = np.array([10, -10, 5, -5, 0])
    if k % 512:
        return np.exp2(np.random.permutation(np.resize(levels, k // 32))).repeat(32)
    a = np.empty((k // 512, 16))
    for p in range(k // 512):
        a[p, :8] = np.random.permutation(np.resize(levels, 8))
        for g in range(8):
            far = levels[np.abs(levels - a[p, g]) >= 10]
            a[p, g + 8] = far[np.random.randint(len(far))]
    return np.exp2(a.ravel()).repeat(32)


def f64(x):
    return np.asarray(x).astype(np.float64)


def striped(idx):
    return np.tile(idx.reshape(-1, 16).T, (8, 1)).astype(np.uint16)


def unstriped(offs):
    return offs[:16].T.reshape(-1).astype(np.int64)


E2M1 = np.array([0.0, 0.5, 1.0, 1.5, 2.0, 3.0, 4.0, 6.0, -0.0, -0.5, -1.0, -1.5, -2.0, -3.0, -4.0, -6.0])


def pack_weight(w, fmt):
    k, n = w.shape
    w = f64(np.asarray(w, np.float32).astype(ml_dtypes.bfloat16)).reshape(k // 32, 32, n)
    amax = np.abs(w).max(1)
    if fmt == "e4m3":
        byte = np.frexp(amax)[1] - 1 + 127 - 7
    else:
        mant, ex = np.frexp(amax / 6.0)
        byte = np.where(mant > 0.5, ex, ex - 1) + 127
    byte = np.clip(np.where(amax > 0, byte, 1), 1, 254)
    scaled = (w * np.exp2(127.0 - byte)[:, None, :]).reshape(k, n).astype(np.float32)
    by_word = np.ascontiguousarray(scaled.reshape(k // 512, 128, 4, n).transpose(0, 1, 3, 2))
    if fmt == "e4m3":
        words = by_word.astype(ml_dtypes.float8_e4m3fn).view(np.uint8)
    else:
        c = by_word.astype(ml_dtypes.float4_e2m1fn).view(np.uint8) & 0xF
        words = (c[..., 0::2] | (c[..., 1::2] << 4)).reshape(k // 512, 128, 2 * n)
    return np.ascontiguousarray(words), np.ascontiguousarray(byte.astype(np.uint8).reshape(k // 512, 16, n))


def unpack_weight(words, scales, fmt):
    g, _, n = scales.shape
    words = np.ascontiguousarray(words).reshape(g, 128, n, -1)
    if fmt == "e4m3":
        vals = words.view(ml_dtypes.float8_e4m3fn).astype(np.float64)
    else:
        nib = np.empty((g, 128, n, 4), np.uint8)
        nib[..., 0::2] = words & 0xF
        nib[..., 1::2] = words >> 4
        vals = E2M1[nib]
    vals = vals * np.repeat(np.exp2(scales.astype(np.float64) - 127.0), 8, axis=1)[..., None]
    return vals.transpose(0, 1, 3, 2).reshape(g * 512, n)


def gelu(v):
    return 0.5 * v * (1.0 + np.tanh(np.sqrt(2.0 / np.pi) * (v + 0.044715 * v**3)))


K, H, N, T, S, T2 = 1536, 512, 512, 4096, 1024, 2048


def setup_inputs():
    n = np.random.standard_normal
    s = mx_kscale(K)[:, None]
    u = mx_kscale(H)[:, None]
    tab_words, tab_scales = pack_weight(n((K, T)) * s, "e4m3")
    wb4_words, wb4_scales = pack_weight(n((K, H)) / s / np.sqrt(K), "e2m1")
    return {
        "tab_words": tab_words,
        "tab_scales": tab_scales,
        "offs": striped(np.random.permutation(T)[:S]),
        "offs2": striped(np.random.permutation(T)[:S]),
        "offs3": striped(np.random.permutation(T2)[:S]),
        "wa": (n((K, H)) / s / np.sqrt(K)).astype(np.float32),
        "wb4_words": wb4_words,
        "wb4_scales": wb4_scales,
        "gain": (np.exp(0.3 * n(H)) * u[:, 0]).astype(np.float32),
        "wc": (1.3 * n((H, N)) / u / np.sqrt(H)).astype(np.float32),
        "wgo": np.exp(0.3 * n((128, S))).astype(np.float32),
    }


def reference(tab_words, tab_scales, offs, offs2, offs3, wa, wb4_words, wb4_scales, gain, wc, wgo):
    TW = unpack_weight(tab_words, tab_scales, "e4m3")
    v = TW[:, unstriped(offs)]
    v2 = TW[:, unstriped(offs2)]
    wb4 = unpack_weight(wb4_words, wb4_scales, "e2m1")
    a = mxq(f64(wa), 0, "e4m3").T @ v
    b = wb4.T @ v2
    z = f64(gain)[:, None] * np.tanh(a + b)
    zq = mxq(z, 0, "e4m3")
    y = mxq(f64(wc), 0, "e4m3").T @ zq
    y = np.abs(y + a)
    out = np.zeros((N, T2))
    out[:, unstriped(offs3)] = np.tile(f64(wgo), (N // 128, 1)) * y
    return out

@@ -1,0 +1,268 @@
+from contextlib import ExitStack
+
+import concourse.mybir as mybir
+from concourse.masks import make_identity
+
+K, H, N, T, S, T2 = 1536, 512, 512, 4096, 1024, 2048
+FLOPS = 2 * (2 * K * H * S + H * N * S)
+
+F32 = mybir.dt.float32
+BF16 = mybir.dt.bfloat16
+I32 = mybir.dt.int32
+U32 = mybir.dt.uint32
+U16 = mybir.dt.uint16
+U8 = mybir.dt.uint8
+FP8X4 = mybir.dt.float8_e4m3fn_x4
+FP4X4 = mybir.dt.float4_e2m1fn_x4
+ACT = mybir.ActivationFunctionType
+MULT = mybir.AluOpType.mult
+
+P = 128
+PACK = 4
+PASSES = K // (P * PACK)
+CHUNKS = S // P
+PAIR = 2 * P
+HALF = S // 2
+
+
+def tile_list_lightpath_route_scores_kernel(
+    tc, tab_words, tab_scales, offs, offs2, offs3, wa, wb4_words, wb4_scales, gain, wc, wgo, out
+):
+    nc = tc.nc
+    with ExitStack() as ctx:
+        keep = ctx.enter_context(tc.tile_pool(name="keep", bufs=1))
+        big = ctx.enter_context(tc.tile_pool(name="big", bufs=PASSES))
+        ring = ctx.enter_context(tc.tile_pool(name="ring", bufs=2))
+        psum = ctx.enter_context(tc.psum_pool(name="psum", bufs=1))
+
+        list_a = keep.tile([P, S // 16], U16, name="list_a")
+        list_b = keep.tile([P, S // 16], U16, name="list_b")
+        list_o = keep.tile([P, S // 16], U16, name="list_o")
+        banks = [psum.tile([P, 512], F32, name=f"bank{i}") for i in range(8)]
+
+        tab_bytes = keep.tile([P, T], U8, name="tab_bytes", align_bytes=64)
+        nc.vector.memset(tab_bytes[0:80, :].bitcast(I32), 0)
+        wb_plane = keep.tile([P, PASSES, H], U8, name="wb_plane", align_bytes=64)
+        nc.vector.memset(wb_plane[:].bitcast(I32), 0)
+        moved = [keep.tile([P, 2 * S], U8, name=f"moved{a}", align_bytes=64) for a in range(PASSES)]
+        for m in moved:
+            nc.vector.memset(m[:].bitcast(I32), 0)
+
+        nc.sync.dma_start(list_b[:], offs2)
+        nc.sync.dma_start(list_a[:], offs)
+        scale_rows = tab_scales.rearrange("a q t -> (a q) t").bitcast(I32)
+        nc.sync.dma_start(tab_bytes[80:96, :].bitcast(I32), scale_rows[0:16, :])
+        nc.sync.dma_start(tab_bytes[96:128, :].bitcast(I32), scale_rows[16:48, :])
+        wb_codes = keep.tile([P, PASSES, 2 * H], U8, name="wb_codes", align_bytes=64)
+        nc.sync.dma_start(wb_codes[:].bitcast(I32), wb4_words.rearrange("a p n -> p a n").bitcast(I32))
+        gain_sb = keep.tile([P, PACK], F32, name="gain_sb")
+        nc.sync.dma_start(gain_sb[:], gain.rearrange("(p t) -> p t", t=PACK))
+        for q in range(4):
+            nc.gpsimd.dma_start(
+                wb_plane[32 * q : 32 * q + 4, :, :].bitcast(I32),
+                wb4_scales[:, 4 * q : 4 * q + 4, :].rearrange("a r n -> r a n").bitcast(I32),
+            )
+        ident = keep.tile([P, P], F32, name="ident")
+        make_identity(nc, ident[:])
+
+        tab = [big.tile([P, T], I32, name=f"tab{a}", tag="big") for a in range(PASSES)]
+
+        def load_tab(a):
+            nc.sync.dma_start(tab[a][:], tab_words[a].rearrange("p n t -> p (n t)").bitcast(I32))
+
+        load_tab(0)
+        load_tab(1)
+        load_tab(2)
+        raw = [keep.tile([P, PACK, H], F32, name=f"raw{a}", tag=f"raw{a}") for a in range(PASSES + 1)]
+        for a in range(PASSES):
+            rows = wa[a * P * PACK : (a + 1) * P * PACK, :]
+            nc.sync.dma_start(raw[a][:], rows.rearrange("(p j) n -> p j n", j=PACK))
+        nc.sync.dma_start(raw[PASSES][:], wc.rearrange("(p j) n -> p j n", j=PACK))
+        nc.sync.dma_start(list_o[:], offs3)
+
+        gain_wide = keep.tile([P, P, PACK], F32, name="gain_wide")
+        nc.scalar.activation(gain_wide[:], gain_sb[:].unsqueeze(1).to_broadcast([P, P, PACK]), ACT.Copy)
+
+        picked = keep.tile([P, 2 * S], U8, name="picked", align_bytes=64)
+        nc.vector.tensor_copy(picked[:, 0:S], tab_bytes[:].indirect(list_b[:]))
+        nc.vector.tensor_copy(picked[:, S : 2 * S], tab_bytes[:].indirect(list_a[:]))
+        for a in range(PASSES):
+            for q in range(4):
+                row = 80 + 16 * a + 4 * q
+                nc.gpsimd.dma_start(
+                    moved[a][32 * q : 32 * q + 4, :].bitcast(I32), picked[row : row + 4, :].bitcast(I32)
+                )
+
+        pages = [keep.tile([P, T2], F32, name=f"page{t}") for t in range(2)]
+        for page in pages:
+            nc.vector.memset(page[:], 0.0)
+
+        words_a = [keep.tile([P, S], U32, name=f"words_a{a}", align_bytes=64) for a in range(PASSES)]
+        words_b = [keep.tile([P, S], U32, name=f"words_b{a}", align_bytes=64) for a in range(PASSES)]
+        for a in range(PASSES):
+            window = tab[a][:].bitcast(U32)
+            for words, lst in ((words_b[a], list_b), (words_a[a], list_a)):
+                if a < PASSES - 1:
+                    nc.vector.tensor_copy(words[:], window.indirect(lst[:]))
+                else:
+                    for h in range(2):
+                        nc.vector.tensor_copy(
+                            words[:, h * HALF : (h + 1) * HALF],
+                            window.indirect(lst[:, h * HALF // 16 : (h + 1) * HALF // 16]),
+                        )
+
+        factors = [big.tile([P, PACK, HALF], F32, name=f"factors{h}", tag="big") for h in range(2)]
+        dealt = wgo.rearrange("(m t) j -> m t j", t=PACK)
+        for h in range(2):
+            for q in (0, 2, 1, 3):
+                nc.sync.dma_start(factors[h][32 * q : 32 * q + 32, :, :], dealt[:, :, h * HALF : (h + 1) * HALF])
+
+        def by_slot(bank):
+            return bank[:].rearrange("p (m t) -> p t m", t=PACK)
+
+        def slots(tile):
+            return tile.rearrange("p (t m) -> p t m", t=PACK)
+
+        b_sb = [raw[c // PACK][:, c % PACK, :] for c in range(CHUNKS)]
+        for a in range(PASSES):
+            for c in range(CHUNKS):
+                cols = slice(c * P, (c + 1) * P)
+                nc.tensor.matmul_mx(
+                    out=banks[c][:],
+                    lhsT=words_b[a][:, cols].bitcast(FP8X4),
+                    lhsT_scale=moved[a][:, cols],
+                    rhs=wb_codes[:, a, :].bitcast(FP4X4),
+                    rhs_scale=wb_plane[:, a, :],
+                    start=(a == 0),
+                    stop=(a == PASSES - 1),
+                )
+
+        codes = [keep.tile([P, H], U32, name=f"codes{a}", align_bytes=64) for a in range(PASSES + 1)]
+        planes = [keep.tile([P, H], U8, name=f"planes{a}", align_bytes=64) for a in range(PASSES + 1)]
+
+        def weave(a, copy):
+            woven = ring.tile([P, H, PACK], BF16, name="woven", align_bytes=64)
+            copy(woven[:], raw[a][:].rearrange("p j c -> p c j"))
+            return woven
+
+        def quantise(a, woven):
+            nc.vector.quantize_mx(
+                out=codes[a][:].bitcast(FP8X4), scales=planes[a][:], in_=woven[:].rearrange("p c j -> p (c j)")
+            )
+
+        woven0 = weave(0, nc.scalar.copy)
+        woven1 = weave(1, nc.vector.tensor_copy)
+        for c in range(CHUNKS):
+            nc.scalar.copy(slots(b_sb[c]), by_slot(banks[c]))
+        quantise(0, woven0)
+        quantise(1, woven1)
+        quantise(2, weave(2, nc.vector.tensor_copy))
+        quantise(3, weave(3, nc.vector.tensor_copy))
+        for t in range(2, PACK):
+            pages.append(keep.tile([P, T2], F32, name=f"page{t}", tag=f"raw{t}"))
+
+        a_banks = banks[0:3]
+        turn_banks = banks[3:8]
+        a_sb = {}
+        y_sb = {}
+        ths = {}
+        zs = {}
+
+        def turn_sum(dst, first, second):
+            nc.tensor.matmul(dst, lhsT=first, rhs=ident[:], is_transpose=True, start=True, stop=False)
+            nc.tensor.matmul(dst, lhsT=second, rhs=ident[:], is_transpose=True, start=False, stop=True)
+
+        def front(c):
+            cols = slice(c * P, (c + 1) * P)
+            bank = a_banks[c % 3]
+            for a in range(PASSES):
+                nc.tensor.matmul_mx(
+                    out=bank[:],
+                    lhsT=words_a[a][:, cols].bitcast(FP8X4),
+                    lhsT_scale=moved[a][:, S + c * P : S + (c + 1) * P],
+                    rhs=codes[a][:].bitcast(FP8X4),
+                    rhs_scale=planes[a][:],
+                    start=(a == 0),
+                    stop=(a == PASSES - 1),
+                )
+            a_sb[c] = ring.tile([P, H], F32, name="a_sb", bufs=8)
+            nc.scalar.copy(slots(a_sb[c][:]), by_slot(bank))
+            bank = turn_banks[c % 5]
+            for t in range(PACK):
+                block = slice(t * P, (t + 1) * P)
+                turn_sum(bank[:, block], b_sb[c][:, block], a_sb[c][:, block])
+            th = ring.tile([P, P, PACK], F32, name="th", bufs=4)
+            nc.scalar.activation(th[:], bank[:].rearrange("p (t j) -> p j t", t=PACK), ACT.Tanh)
+            ths[c] = th
+
+        def middle(c):
+            th = ths[c]
+            z = ring.tile([P, P * PACK], BF16, name="z", align_bytes=64)
+            nc.vector.tensor_tensor(
+                z[:], th[:].rearrange("p j t -> p (j t)"), gain_wide[:].rearrange("p j t -> p (j t)"), MULT
+            )
+            z_codes = ring.tile([P, P], U32, name="z_codes", align_bytes=64)
+            z_plane = ring.tile([P, P], U8, name="z_plane", align_bytes=64)
+            nc.vector.quantize_mx(out=z_codes[:].bitcast(FP8X4), scales=z_plane[:], in_=z[:])
+            zs[c] = (z_codes, z_plane)
+
+        def second(c, y_bank):
+            z_codes, z_plane = zs[c]
+            nc.tensor.matmul_mx(
+                out=y_bank[:],
+                lhsT=z_codes[:].bitcast(FP8X4),
+                lhsT_scale=z_plane[:],
+                rhs=codes[PASSES][:].bitcast(FP8X4),
+                rhs_scale=planes[PASSES][:],
+                start=True,
+                stop=True,
+            )
+            y_sb[c] = ring.tile([P, N], F32, name="y_sb", bufs=6)
+            nc.scalar.copy(slots(y_sb[c][:]), by_slot(y_bank))
+
+        def back(parts, bank):
+            at = 0
+            for t, chunks in parts:
+                block = slice(t * P, (t + 1) * P)
+                for c in chunks:
+                    turn_sum(bank[:, at : at + P], a_sb[c][:, block], y_sb[c][:, block])
+                    at += P
+            size = ring.tile([P, 4 * P], F32, name="size", bufs=3)
+            nc.scalar.activation(size[:], bank[:], ACT.Abs)
+            at = 0
+            for t, chunks in parts:
+                first, width = chunks[0] * P, len(chunks) * P
+                nc.vector.tensor_tensor(
+                    pages[t][:].indirect(list_o[:, first // 16 : (first + width) // 16]),
+                    size[:, at : at + width],
+                    factors[first // HALF][:, t, first % HALF : first % HALF + width],
+                    MULT,
+                )
+                at += width
+                if chunks[-1] == CHUNKS - 1:
+                    nc.sync.dma_start(out.rearrange("(p t) c -> t p c", t=PACK)[t], pages[t][:])
+
+        steps = [[(t, (2 * pair, 2 * pair + 1)) for t in (2 * u, 2 * u + 1)] for pair in range(2) for u in range(2)]
+        steps += [[(t, (2 * pair, 2 * pair + 1)) for t in (0, 1)] for pair in (2, 3)]
+        steps += [[(t, (4, 5, 6, 7))] for t in (2, 3)]
+        ahead = [[2], [3], [4, 5], [6], [7], [], [], []]
+        step_banks = [turn_banks[i] for i in (2, 3, 0, 1, 2, 3, 4, 0)]
+
+        for c in range(2):
+            front(c)
+        for c in range(2):
+            middle(c)
+            second(c, turn_banks[c])
+        for t in range(2, PACK):
+            for h in range(2):
+                nc.vector.memset(pages[t][:, h * S : (h + 1) * S], 0.0)
+        front(2)
+        for k, parts in enumerate(steps):
+            for c in ahead[k]:
+                middle(c)
+            back(parts, step_banks[k])
+            if k + 1 < len(steps):
+                for c in ahead[k + 1]:
+                    front(c)
+            for c in ahead[k]:
+                second(c, step_banks[k])

@@ -23,6 +23,7 @@ PASSES = K // (P * PACK)
 CHUNKS = S // P
 PAIR = 2 * P
 HALF = S // 2
+ON_SCALAR = 6
 
 
 def tile_list_lightpath_route_scores_kernel(
@@ -31,7 +32,7 @@ def tile_list_lightpath_route_scores_kernel(
     nc = tc.nc
     with ExitStack() as ctx:
         keep = ctx.enter_context(tc.tile_pool(name="keep", bufs=1))
-        big = ctx.enter_context(tc.tile_pool(name="big", bufs=PASSES))
+        big = ctx.enter_context(tc.tile_pool(name="big", bufs=1))
         ring = ctx.enter_context(tc.tile_pool(name="ring", bufs=2))
         psum = ctx.enter_context(tc.psum_pool(name="psum", bufs=1))
 
@@ -41,9 +42,9 @@ def tile_list_lightpath_route_scores_kernel(
         banks = [psum.tile([P, 512], F32, name=f"bank{i}") for i in range(8)]
 
         tab_bytes = keep.tile([P, T], U8, name="tab_bytes", align_bytes=64)
-        nc.vector.memset(tab_bytes[0:80, :].bitcast(I32), 0)
         wb_plane = keep.tile([P, PASSES, H], U8, name="wb_plane", align_bytes=64)
         nc.vector.memset(wb_plane[:].bitcast(I32), 0)
+        nc.vector.memset(tab_bytes[0:80, :].bitcast(I32), 0)
         moved = [keep.tile([P, 2 * S], U8, name=f"moved{a}", align_bytes=64) for a in range(PASSES)]
         for m in moved:
             nc.vector.memset(m[:].bitcast(I32), 0)
@@ -53,37 +54,36 @@ def tile_list_lightpath_route_scores_kernel(
         scale_rows = tab_scales.rearrange("a q t -> (a q) t").bitcast(I32)
         nc.sync.dma_start(tab_bytes[80:96, :].bitcast(I32), scale_rows[0:16, :])
         nc.sync.dma_start(tab_bytes[96:128, :].bitcast(I32), scale_rows[16:48, :])
-        wb_codes = keep.tile([P, PASSES, 2 * H], U8, name="wb_codes", align_bytes=64)
-        nc.sync.dma_start(wb_codes[:].bitcast(I32), wb4_words.rearrange("a p n -> p a n").bitcast(I32))
-        gain_sb = keep.tile([P, PACK], F32, name="gain_sb")
-        nc.sync.dma_start(gain_sb[:], gain.rearrange("(p t) -> p t", t=PACK))
-        for q in range(4):
-            nc.gpsimd.dma_start(
-                wb_plane[32 * q : 32 * q + 4, :, :].bitcast(I32),
-                wb4_scales[:, 4 * q : 4 * q + 4, :].rearrange("a r n -> r a n").bitcast(I32),
-            )
-        ident = keep.tile([P, P], F32, name="ident")
-        make_identity(nc, ident[:])
-
-        tab = [big.tile([P, T], I32, name=f"tab{a}", tag="big") for a in range(PASSES)]
+        tab = [big.tile([P, T], I32, name=f"tab{a}", offset=a * 4 * T) for a in range(PASSES)]
 
         def load_tab(a):
             nc.sync.dma_start(tab[a][:], tab_words[a].rearrange("p n t -> p (n t)").bitcast(I32))
 
         load_tab(0)
+        wb_codes = keep.tile([P, PASSES, 2 * H], U8, name="wb_codes", align_bytes=64)
+        nc.sync.dma_start(wb_codes[:].bitcast(I32), wb4_words.rearrange("a p n -> p a n").bitcast(I32))
+        gain_sb = keep.tile([P, PACK], F32, name="gain_sb")
+        nc.sync.dma_start(gain_sb[:], gain.rearrange("(p t) -> p t", t=PACK))
+        nc.sync.dma_start(list_o[:], offs3)
+        for q in range(4):
+            nc.sync.dma_start(
+                wb_plane[32 * q : 32 * q + 4, :, :].bitcast(I32),
+                wb4_scales[:, 4 * q : 4 * q + 4, :].rearrange("a r n -> r a n").bitcast(I32),
+            )
         load_tab(1)
         load_tab(2)
-        raw = [keep.tile([P, PACK, H], F32, name=f"raw{a}", tag=f"raw{a}") for a in range(PASSES + 1)]
+        raw = [big.tile([P, PACK, H], F32, name=f"raw{a}", offset=(6 + a) * 2 * T) for a in range(PASSES + 1)]
         for a in range(PASSES):
             rows = wa[a * P * PACK : (a + 1) * P * PACK, :]
             nc.sync.dma_start(raw[a][:], rows.rearrange("(p j) n -> p j n", j=PACK))
         nc.sync.dma_start(raw[PASSES][:], wc.rearrange("(p j) n -> p j n", j=PACK))
-        nc.sync.dma_start(list_o[:], offs3)
+        ident = keep.tile([P, P], F32, name="ident")
+        make_identity(nc, ident[:])
 
         gain_wide = keep.tile([P, P, PACK], F32, name="gain_wide")
         nc.scalar.activation(gain_wide[:], gain_sb[:].unsqueeze(1).to_broadcast([P, P, PACK]), ACT.Copy)
 
-        picked = keep.tile([P, 2 * S], U8, name="picked", align_bytes=64)
+        picked = big.tile([P, 2 * S], U8, name="picked", offset=10 * 2 * T)
         nc.vector.tensor_copy(picked[:, 0:S], tab_bytes[:].indirect(list_b[:]))
         nc.vector.tensor_copy(picked[:, S : 2 * S], tab_bytes[:].indirect(list_a[:]))
         for a in range(PASSES):
@@ -93,9 +93,9 @@ def tile_list_lightpath_route_scores_kernel(
                     moved[a][32 * q : 32 * q + 4, :].bitcast(I32), picked[row : row + 4, :].bitcast(I32)
                 )
 
-        pages = [keep.tile([P, T2], F32, name=f"page{t}") for t in range(2)]
-        for page in pages:
-            nc.vector.memset(page[:], 0.0)
+        pages = [keep.tile([P, T2], F32, name="page0"), big.tile([P, T2], F32, name="page1", offset=10 * 2 * T)]
+        nc.vector.memset(pages[0][:], 0.0)
+        nc.gpsimd.memset(pages[1][:], 0.0)
 
         words_a = [keep.tile([P, S], U32, name=f"words_a{a}", align_bytes=64) for a in range(PASSES)]
         words_b = [keep.tile([P, S], U32, name=f"words_b{a}", align_bytes=64) for a in range(PASSES)]
@@ -111,17 +111,17 @@ def tile_list_lightpath_route_scores_kernel(
                             window.indirect(lst[:, h * HALF // 16 : (h + 1) * HALF // 16]),
                         )
 
-        factors = [big.tile([P, PACK, HALF], F32, name=f"factors{h}", tag="big") for h in range(2)]
+        factors = [big.tile([P, PACK, HALF], F32, name=f"factors{h}", offset=h * 2 * T) for h in range(2)]
         dealt = wgo.rearrange("(m t) j -> m t j", t=PACK)
         for h in range(2):
             for q in (0, 2, 1, 3):
                 nc.sync.dma_start(factors[h][32 * q : 32 * q + 32, :, :], dealt[:, :, h * HALF : (h + 1) * HALF])
 
         def by_slot(bank):
-            return bank[:].rearrange("p (m t) -> p t m", t=PACK)
+            return bank[:].rearrange("p (m t) -> p m t", t=PACK)
 
         def slots(tile):
-            return tile.rearrange("p (t m) -> p t m", t=PACK)
+            return tile.rearrange("p (t m) -> p m t", t=PACK)
 
         b_sb = [raw[c // PACK][:, c % PACK, :] for c in range(CHUNKS)]
         for a in range(PASSES):
@@ -159,7 +159,7 @@ def tile_list_lightpath_route_scores_kernel(
         quantise(2, weave(2, nc.vector.tensor_copy))
         quantise(3, weave(3, nc.vector.tensor_copy))
         for t in range(2, PACK):
-            pages.append(keep.tile([P, T2], F32, name=f"page{t}", tag=f"raw{t}"))
+            pages.append(big.tile([P, T2], F32, name=f"page{t}", offset=(6 + t) * 2 * T))
 
         a_banks = banks[0:3]
         turn_banks = banks[3:8]
@@ -191,16 +191,27 @@ def tile_list_lightpath_route_scores_kernel(
             for t in range(PACK):
                 block = slice(t * P, (t + 1) * P)
                 turn_sum(bank[:, block], b_sb[c][:, block], a_sb[c][:, block])
-            th = ring.tile([P, P, PACK], F32, name="th", bufs=4)
-            nc.scalar.activation(th[:], bank[:].rearrange("p (t j) -> p j t", t=PACK), ACT.Tanh)
+            th = ring.tile([P, H], F32, name="th", bufs=4)
+            if c < ON_SCALAR:
+                nc.scalar.activation(
+                    th[:].rearrange("p (j t) -> p j t", t=PACK), bank[:].rearrange("p (t j) -> p j t", t=PACK), ACT.Tanh
+                )
+            else:
+                nc.scalar.activation(th[:], bank[:], ACT.Tanh)
             ths[c] = th
 
         def middle(c):
             th = ths[c]
             z = ring.tile([P, P * PACK], BF16, name="z", align_bytes=64)
-            nc.vector.tensor_tensor(
-                z[:], th[:].rearrange("p j t -> p (j t)"), gain_wide[:].rearrange("p j t -> p (j t)"), MULT
-            )
+            if c < ON_SCALAR:
+                nc.vector.tensor_tensor(z[:], th[:], gain_wide[:].rearrange("p j t -> p (j t)"), MULT)
+            else:
+                flat = ring.tile([P, PACK, P], BF16, name="flat")
+                for t in range(PACK):
+                    nc.scalar.activation(
+                        flat[:, t, :], th[:, t * P : (t + 1) * P], ACT.Copy, scale=gain_sb[:, t : t + 1]
+                    )
+                nc.scalar.copy(z[:].rearrange("p (j t) -> p j t", t=PACK), flat[:].rearrange("p t j -> p j t"))
             z_codes = ring.tile([P, P], U32, name="z_codes", align_bytes=64)
             z_plane = ring.tile([P, P], U8, name="z_plane", align_bytes=64)
             nc.vector.quantize_mx(out=z_codes[:].bitcast(FP8X4), scales=z_plane[:], in_=z[:])

from contextlib import ExitStack

import concourse.mybir as mybir
from concourse.masks import make_identity

K, H, N, T, S, T2 = 1536, 512, 512, 4096, 1024, 2048
FLOPS = 2 * (2 * K * H * S + H * N * S)

F32 = mybir.dt.float32
BF16 = mybir.dt.bfloat16
I32 = mybir.dt.int32
U32 = mybir.dt.uint32
U16 = mybir.dt.uint16
U8 = mybir.dt.uint8
FP8X4 = mybir.dt.float8_e4m3fn_x4
FP4X4 = mybir.dt.float4_e2m1fn_x4
ACT = mybir.ActivationFunctionType
MULT = mybir.AluOpType.mult

P = 128
PACK = 4
PASSES = K // (P * PACK)
CHUNKS = S // P
PAIR = 2 * P
HALF = S // 2
ON_SCALAR = 6


def tile_list_lightpath_route_scores_kernel(
    tc, tab_words, tab_scales, offs, offs2, offs3, wa, wb4_words, wb4_scales, gain, wc, wgo, out
):
    nc = tc.nc
    with ExitStack() as ctx:
        keep = ctx.enter_context(tc.tile_pool(name="keep", bufs=1))
        big = ctx.enter_context(tc.tile_pool(name="big", bufs=1))
        ring = ctx.enter_context(tc.tile_pool(name="ring", bufs=2))
        psum = ctx.enter_context(tc.psum_pool(name="psum", bufs=1))

        list_a = keep.tile([P, S // 16], U16, name="list_a")
        list_b = keep.tile([P, S // 16], U16, name="list_b")
        list_o = keep.tile([P, S // 16], U16, name="list_o")
        banks = [psum.tile([P, 512], F32, name=f"bank{i}") for i in range(8)]

        tab_bytes = keep.tile([P, T], U8, name="tab_bytes", align_bytes=64)
        wb_plane = keep.tile([P, PASSES, H], U8, name="wb_plane", align_bytes=64)
        nc.vector.memset(wb_plane[:].bitcast(I32), 0)
        nc.vector.memset(tab_bytes[0:80, :].bitcast(I32), 0)
        moved = [keep.tile([P, 2 * S], U8, name=f"moved{a}", align_bytes=64) for a in range(PASSES)]
        for m in moved:
            nc.vector.memset(m[:].bitcast(I32), 0)

        nc.sync.dma_start(list_b[:], offs2)
        nc.sync.dma_start(list_a[:], offs)
        scale_rows = tab_scales.rearrange("a q t -> (a q) t").bitcast(I32)
        nc.sync.dma_start(tab_bytes[80:96, :].bitcast(I32), scale_rows[0:16, :])
        nc.sync.dma_start(tab_bytes[96:128, :].bitcast(I32), scale_rows[16:48, :])
        tab = [big.tile([P, T], I32, name=f"tab{a}", offset=a * 4 * T) for a in range(PASSES)]

        def load_tab(a):
            nc.sync.dma_start(tab[a][:], tab_words[a].rearrange("p n t -> p (n t)").bitcast(I32))

        load_tab(0)
        wb_codes = keep.tile([P, PASSES, 2 * H], U8, name="wb_codes", align_bytes=64)
        nc.sync.dma_start(wb_codes[:].bitcast(I32), wb4_words.rearrange("a p n -> p a n").bitcast(I32))
        gain_sb = keep.tile([P, PACK], F32, name="gain_sb")
        nc.sync.dma_start(gain_sb[:], gain.rearrange("(p t) -> p t", t=PACK))
        nc.sync.dma_start(list_o[:], offs3)
        for q in range(4):
            nc.sync.dma_start(
                wb_plane[32 * q : 32 * q + 4, :, :].bitcast(I32),
                wb4_scales[:, 4 * q : 4 * q + 4, :].rearrange("a r n -> r a n").bitcast(I32),
            )
        load_tab(1)
        load_tab(2)
        raw = [big.tile([P, PACK, H], F32, name=f"raw{a}", offset=(6 + a) * 2 * T) for a in range(PASSES + 1)]
        for a in range(PASSES):
            rows = wa[a * P * PACK : (a + 1) * P * PACK, :]
            nc.sync.dma_start(raw[a][:], rows.rearrange("(p j) n -> p j n", j=PACK))
        nc.sync.dma_start(raw[PASSES][:], wc.rearrange("(p j) n -> p j n", j=PACK))
        ident = keep.tile([P, P], F32, name="ident")
        make_identity(nc, ident[:])

        gain_wide = keep.tile([P, P, PACK], F32, name="gain_wide")
        nc.scalar.activation(gain_wide[:], gain_sb[:].unsqueeze(1).to_broadcast([P, P, PACK]), ACT.Copy)

        picked = big.tile([P, 2 * S], U8, name="picked", offset=10 * 2 * T)
        nc.vector.tensor_copy(picked[:, 0:S], tab_bytes[:].indirect(list_b[:]))
        nc.vector.tensor_copy(picked[:, S : 2 * S], tab_bytes[:].indirect(list_a[:]))
        for a in range(PASSES):
            for q in range(4):
                row = 80 + 16 * a + 4 * q
                nc.gpsimd.dma_start(
                    moved[a][32 * q : 32 * q + 4, :].bitcast(I32), picked[row : row + 4, :].bitcast(I32)
                )

        pages = [keep.tile([P, T2], F32, name="page0"), big.tile([P, T2], F32, name="page1", offset=10 * 2 * T)]
        nc.vector.memset(pages[0][:], 0.0)
        nc.gpsimd.memset(pages[1][:], 0.0)

        words_a = [keep.tile([P, S], U32, name=f"words_a{a}", align_bytes=64) for a in range(PASSES)]
        words_b = [keep.tile([P, S], U32, name=f"words_b{a}", align_bytes=64) for a in range(PASSES)]
        for a in range(PASSES):
            window = tab[a][:].bitcast(U32)
            for words, lst in ((words_b[a], list_b), (words_a[a], list_a)):
                if a < PASSES - 1:
                    nc.vector.tensor_copy(words[:], window.indirect(lst[:]))
                else:
                    for h in range(2):
                        nc.vector.tensor_copy(
                            words[:, h * HALF : (h + 1) * HALF],
                            window.indirect(lst[:, h * HALF // 16 : (h + 1) * HALF // 16]),
                        )

        factors = [big.tile([P, PACK, HALF], F32, name=f"factors{h}", offset=h * 2 * T) for h in range(2)]
        dealt = wgo.rearrange("(m t) j -> m t j", t=PACK)
        for h in range(2):
            for q in (0, 2, 1, 3):
                nc.sync.dma_start(factors[h][32 * q : 32 * q + 32, :, :], dealt[:, :, h * HALF : (h + 1) * HALF])

        def by_slot(bank):
            return bank[:].rearrange("p (m t) -> p m t", t=PACK)

        def slots(tile):
            return tile.rearrange("p (t m) -> p m t", t=PACK)

        b_sb = [raw[c // PACK][:, c % PACK, :] for c in range(CHUNKS)]
        for a in range(PASSES):
            for c in range(CHUNKS):
                cols = slice(c * P, (c + 1) * P)
                nc.tensor.matmul_mx(
                    out=banks[c][:],
                    lhsT=words_b[a][:, cols].bitcast(FP8X4),
                    lhsT_scale=moved[a][:, cols],
                    rhs=wb_codes[:, a, :].bitcast(FP4X4),
                    rhs_scale=wb_plane[:, a, :],
                    start=(a == 0),
                    stop=(a == PASSES - 1),
                )

        codes = [keep.tile([P, H], U32, name=f"codes{a}", align_bytes=64) for a in range(PASSES + 1)]
        planes = [keep.tile([P, H], U8, name=f"planes{a}", align_bytes=64) for a in range(PASSES + 1)]

        def weave(a, copy):
            woven = ring.tile([P, H, PACK], BF16, name="woven", align_bytes=64)
            copy(woven[:], raw[a][:].rearrange("p j c -> p c j"))
            return woven

        def quantise(a, woven):
            nc.vector.quantize_mx(
                out=codes[a][:].bitcast(FP8X4), scales=planes[a][:], in_=woven[:].rearrange("p c j -> p (c j)")
            )

        woven0 = weave(0, nc.scalar.copy)
        woven1 = weave(1, nc.vector.tensor_copy)
        for c in range(CHUNKS):
            nc.scalar.copy(slots(b_sb[c]), by_slot(banks[c]))
        quantise(0, woven0)
        quantise(1, woven1)
        quantise(2, weave(2, nc.vector.tensor_copy))
        quantise(3, weave(3, nc.vector.tensor_copy))
        for t in range(2, PACK):
            pages.append(big.tile([P, T2], F32, name=f"page{t}", offset=(6 + t) * 2 * T))

        a_banks = banks[0:3]
        turn_banks = banks[3:8]
        a_sb = {}
        y_sb = {}
        ths = {}
        zs = {}

        def turn_sum(dst, first, second):
            nc.tensor.matmul(dst, lhsT=first, rhs=ident[:], is_transpose=True, start=True, stop=False)
            nc.tensor.matmul(dst, lhsT=second, rhs=ident[:], is_transpose=True, start=False, stop=True)

        def front(c):
            cols = slice(c * P, (c + 1) * P)
            bank = a_banks[c % 3]
            for a in range(PASSES):
                nc.tensor.matmul_mx(
                    out=bank[:],
                    lhsT=words_a[a][:, cols].bitcast(FP8X4),
                    lhsT_scale=moved[a][:, S + c * P : S + (c + 1) * P],
                    rhs=codes[a][:].bitcast(FP8X4),
                    rhs_scale=planes[a][:],
                    start=(a == 0),
                    stop=(a == PASSES - 1),
                )
            a_sb[c] = ring.tile([P, H], F32, name="a_sb", bufs=8)
            nc.scalar.copy(slots(a_sb[c][:]), by_slot(bank))
            bank = turn_banks[c % 5]
            for t in range(PACK):
                block = slice(t * P, (t + 1) * P)
                turn_sum(bank[:, block], b_sb[c][:, block], a_sb[c][:, block])
            th = ring.tile([P, H], F32, name="th", bufs=4)
            if c < ON_SCALAR:
                nc.scalar.activation(
                    th[:].rearrange("p (j t) -> p j t", t=PACK), bank[:].rearrange("p (t j) -> p j t", t=PACK), ACT.Tanh
                )
            else:
                nc.scalar.activation(th[:], bank[:], ACT.Tanh)
            ths[c] = th

        def middle(c):
            th = ths[c]
            z = ring.tile([P, P * PACK], BF16, name="z", align_bytes=64)
            if c < ON_SCALAR:
                nc.vector.tensor_tensor(z[:], th[:], gain_wide[:].rearrange("p j t -> p (j t)"), MULT)
            else:
                flat = ring.tile([P, PACK, P], BF16, name="flat")
                for t in range(PACK):
                    nc.scalar.activation(
                        flat[:, t, :], th[:, t * P : (t + 1) * P], ACT.Copy, scale=gain_sb[:, t : t + 1]
                    )
                nc.scalar.copy(z[:].rearrange("p (j t) -> p j t", t=PACK), flat[:].rearrange("p t j -> p j t"))
            z_codes = ring.tile([P, P], U32, name="z_codes", align_bytes=64)
            z_plane = ring.tile([P, P], U8, name="z_plane", align_bytes=64)
            nc.vector.quantize_mx(out=z_codes[:].bitcast(FP8X4), scales=z_plane[:], in_=z[:])
            zs[c] = (z_codes, z_plane)

        def second(c, y_bank):
            z_codes, z_plane = zs[c]
            nc.tensor.matmul_mx(
                out=y_bank[:],
                lhsT=z_codes[:].bitcast(FP8X4),
                lhsT_scale=z_plane[:],
                rhs=codes[PASSES][:].bitcast(FP8X4),
                rhs_scale=planes[PASSES][:],
                start=True,
                stop=True,
            )
            y_sb[c] = ring.tile([P, N], F32, name="y_sb", bufs=6)
            nc.scalar.copy(slots(y_sb[c][:]), by_slot(y_bank))

        def back(parts, bank):
            at = 0
            for t, chunks in parts:
                block = slice(t * P, (t + 1) * P)
                for c in chunks:
                    turn_sum(bank[:, at : at + P], a_sb[c][:, block], y_sb[c][:, block])
                    at += P
            size = ring.tile([P, 4 * P], F32, name="size", bufs=3)
            nc.scalar.activation(size[:], bank[:], ACT.Abs)
            at = 0
            for t, chunks in parts:
                first, width = chunks[0] * P, len(chunks) * P
                nc.vector.tensor_tensor(
                    pages[t][:].indirect(list_o[:, first // 16 : (first + width) // 16]),
                    size[:, at : at + width],
                    factors[first // HALF][:, t, first % HALF : first % HALF + width],
                    MULT,
                )
                at += width
                if chunks[-1] == CHUNKS - 1:
                    nc.sync.dma_start(out.rearrange("(p t) c -> t p c", t=PACK)[t], pages[t][:])

        steps = [[(t, (2 * pair, 2 * pair + 1)) for t in (2 * u, 2 * u + 1)] for pair in range(2) for u in range(2)]
        steps += [[(t, (2 * pair, 2 * pair + 1)) for t in (0, 1)] for pair in (2, 3)]
        steps += [[(t, (4, 5, 6, 7))] for t in (2, 3)]
        ahead = [[2], [3], [4, 5], [6], [7], [], [], []]
        step_banks = [turn_banks[i] for i in (2, 3, 0, 1, 2, 3, 4, 0)]

        for c in range(2):
            front(c)
        for c in range(2):
            middle(c)
            second(c, turn_banks[c])
        for t in range(2, PACK):
            for h in range(2):
                nc.vector.memset(pages[t][:, h * S : (h + 1) * S], 0.0)
        front(2)
        for k, parts in enumerate(steps):
            for c in ahead[k]:
                middle(c)
            back(parts, step_banks[k])
            if k + 1 < len(steps):
                for c in ahead[k + 1]:
                    front(c)
            for c in ahead[k]:
                second(c, step_banks[k])
